import numpy as np
import ml_dtypes


def mxq(x, axis, fmt="e4m3"):
    dtype, down = {"e4m3": (ml_dtypes.float8_e4m3fn, 7), "e5m2": (ml_dtypes.float8_e5m2, 14)}[fmt]
    v = np.moveaxis(np.asarray(x, np.float32).astype(ml_dtypes.bfloat16).astype(np.float64), axis, -1)
    blocks = v.reshape(v.shape[:-1] + (-1, 32))
    amax = np.abs(blocks).max(-1, keepdims=True)
    byte = np.maximum(np.where(amax > 0, np.frexp(amax)[1] - 1 + 127, 0) - down, 1)
    scale = np.exp2(byte - 127.0)
    codes = (blocks / scale).astype(np.float32).astype(dtype).astype(np.float64)
    return np.moveaxis((codes * scale).reshape(v.shape), -1, axis)


WIDE = False


def mx_kscale(k):
    if not WIDE:
        return np.ones(k)
    levels = np.array([10, -10, 5, -5, 0])
    if k % 512:
        return np.exp2(np.random.permutation(np.resize(levels, k // 32))).repeat(32)
    a = np.empty((k // 512, 16))
    for p in range(k // 512):
        a[p, :8] = np.random.permutation(np.resize(levels, 8))
        for g in range(8):
            far = levels[np.abs(levels - a[p, g]) >= 10]
            a[p, g + 8] = far[np.random.randint(len(far))]
    return np.exp2(a.ravel()).repeat(32)


def f64(x):
    return np.asarray(x).astype(np.float64)


def striped(idx):
    return np.tile(idx.reshape(-1, 16).T, (8, 1)).astype(np.uint16)


def unstriped(offs):
    return offs[:16].T.reshape(-1).astype(np.int64)


E2M1 = np.array([0.0, 0.5, 1.0, 1.5, 2.0, 3.0, 4.0, 6.0, -0.0, -0.5, -1.0, -1.5, -2.0, -3.0, -4.0, -6.0])


def pack_weight(w, fmt):
    k, n = w.shape
    w = f64(np.asarray(w, np.float32).astype(ml_dtypes.bfloat16)).reshape(k // 32, 32, n)
    amax = np.abs(w).max(1)
    if fmt == "e4m3":
        byte = np.frexp(amax)[1] - 1 + 127 - 7
    else:
        mant, ex = np.frexp(amax / 6.0)
        byte = np.where(mant > 0.5, ex, ex - 1) + 127
    byte = np.clip(np.where(amax > 0, byte, 1), 1, 254)
    scaled = (w * np.exp2(127.0 - byte)[:, None, :]).reshape(k, n).astype(np.float32)
    by_word = np.ascontiguousarray(scaled.reshape(k // 512, 128, 4, n).transpose(0, 1, 3, 2))
    if fmt == "e4m3":
        words = by_word.astype(ml_dtypes.float8_e4m3fn).view(np.uint8)
    else:
        c = by_word.astype(ml_dtypes.float4_e2m1fn).view(np.uint8) & 0xF
        words = (c[..., 0::2] | (c[..., 1::2] << 4)).reshape(k // 512, 128, 2 * n)
    return np.ascontiguousarray(words), np.ascontiguousarray(byte.astype(np.uint8).reshape(k // 512, 16, n))


def unpack_weight(words, scales, fmt):
    g, _, n = scales.shape
    words = np.ascontiguousarray(words).reshape(g, 128, n, -1)
    if fmt == "e4m3":
        vals = words.view(ml_dtypes.float8_e4m3fn).astype(np.float64)
    else:
        nib = np.empty((g, 128, n, 4), np.uint8)
        nib[..., 0::2] = words & 0xF
        nib[..., 1::2] = words >> 4
        vals = E2M1[nib]
    vals = vals * np.repeat(np.exp2(scales.astype(np.float64) - 127.0), 8, axis=1)[..., None]
    return vals.transpose(0, 1, 3, 2).reshape(g * 512, n)


def gelu(v):
    return 0.5 * v * (1.0 + np.tanh(np.sqrt(2.0 / np.pi) * (v + 0.044715 * v**3)))


K, H, N, T, S, P1, P2, P3 = 512, 1024, 768, 4096, 2048, 1024, 512, 256


def setup_inputs():
    n = np.random.standard_normal
    s = mx_kscale(K)[:, None]
    u = mx_kscale(H)[:, None]
    tab_words, tab_scales = pack_weight(n((K, T)) * s, "e4m3")
    wsq_words, wsq_scales = pack_weight(0.9 / np.sqrt(H) * n((H, N)) / u, "e2m1")
    return {
        "tab_words": tab_words, "tab_scales": tab_scales,
        "offs": striped(np.random.permutation(T)[:S]),
        "pos1": striped(np.random.permutation(S)[:P1]),
        "pos2": striped(np.random.permutation(S)[:P1]),
        "pos3": striped(np.random.permutation(P1)[:P2]),
        "pos4": striped(np.random.permutation(P1)[:P2]),
        "pos5": striped(np.random.permutation(P2)[:P3]),
        "pos6": striped(np.random.permutation(P2)[:P3]),
        "w1": (1.4 / np.sqrt(K) * n((K, H)) / s).astype(np.float32),
        "gain": (2.0 * np.exp(0.3 * n(H)) * u[:, 0]).astype(np.float32),
        "wsq_words": wsq_words, "wsq_scales": wsq_scales,
        "wrec": (0.9 / np.sqrt(H) * n((H, N)) / u).astype(np.float32),
    }


def reference(tab_words, tab_scales, offs, pos1, pos2, pos3, pos4, pos5, pos6,
              w1, gain, wsq_words, wsq_scales, wrec):
    v = unpack_weight(tab_words, tab_scales, "e4m3")[:, unstriped(offs)]
    wsq = unpack_weight(wsq_words, wsq_scales, "e2m1")
    h = np.tanh(mxq(f64(w1), 0, "e4m3").T @ v)
    a1 = np.maximum(h[:, unstriped(pos1)], h[:, unstriped(pos2)])
    a2 = f64(gain)[:, None] * (a1[:, unstriped(pos3)] * a1[:, unstriped(pos4)])
    first = a2[:, unstriped(pos5)]
    a3 = np.abs(first - a2[:, unstriped(pos6)])
    y = wsq.T @ mxq(a3, 0, "e4m3") + mxq(f64(wrec), 0, "e4m3").T @ mxq(first, 0, "e4m3")
    return np.tanh(y)

@@ -1,0 +1,279 @@
+from contextlib import ExitStack
+
+import concourse.mybir as mybir
+
+K, H, N, T, S, P1, P2, P3 = 512, 1024, 768, 4096, 2048, 1024, 512, 256
+FLOPS = 2 * K * H * S + 2 * 2 * H * N * P3
+
+F32 = mybir.dt.float32
+BF16 = mybir.dt.bfloat16
+I32 = mybir.dt.int32
+U32 = mybir.dt.uint32
+U16 = mybir.dt.uint16
+U8 = mybir.dt.uint8
+FP8X4 = mybir.dt.float8_e4m3fn_x4
+FP4X4 = mybir.dt.float4_e2m1fn_x4
+ALU = mybir.AluOpType
+ACT = mybir.ActivationFunctionType
+
+P = 128
+PACK = 4
+K_PASS = P * PACK
+BANK = 512
+R_PASSES = H // K_PASS
+SLICES = R_PASSES * PACK
+N_TILES = N // P
+W1_CHUNK = 256
+WREC_CHUNK = 384
+H_SLOTS = 3
+
+
+def tile_list_academy_squad_trials_kernel(
+    tc, tab_words, tab_scales, offs, pos1, pos2, pos3, pos4, pos5, pos6, w1, gain, wsq_words, wsq_scales, wrec, out
+):
+    nc = tc.nc
+    with ExitStack() as ctx:
+        lists = ctx.enter_context(tc.tile_pool(name="lists", bufs=1))
+        keep = ctx.enter_context(tc.tile_pool(name="keep", bufs=1))
+        ring = ctx.enter_context(tc.tile_pool(name="ring", bufs=2))
+        slots = ctx.enter_context(tc.tile_pool(name="slots", bufs=1))
+        head = ctx.enter_context(tc.tile_pool(name="head", bufs=1))
+        h_psum = ctx.enter_context(tc.psum_pool(name="h_psum", bufs=2))
+        y_psum = ctx.enter_context(tc.psum_pool(name="y_psum", bufs=1))
+
+        def load_list(name, src):
+            t = lists.tile(list(src.shape), U16, name=name)
+            nc.sync.dma_start(t[:], src)
+            return t
+
+        table_scales = head.tile([P, T], U8, name="table_scales", align_bytes=64, offset=4 * S - T // 2)
+        nc.vector.memset(table_scales[:].bitcast(I32), 0)
+        offs_t = load_list("offs_t", offs)
+        for q in range(4):
+            nc.scalar.dma_start(
+                table_scales[32 * q : 32 * q + 4, :].bitcast(I32), tab_scales[0, 4 * q : 4 * q + 4, :].bitcast(I32)
+            )
+        w1_raw = []
+
+        def load_w1(c):
+            raw = keep.tile([P, PACK, W1_CHUNK], F32, name="w1_raw%d" % c)
+            nc.sync.dma_start(raw[:], w1[:, c * W1_CHUNK : (c + 1) * W1_CHUNK].rearrange("(p j) c -> p j c", j=PACK))
+            w1_raw.append(raw)
+
+        load_w1(0)
+        load_w1(1)
+        table_words = keep.tile([P, T], I32, name="table_words", align_bytes=64)
+        nc.sync.dma_start(table_words[:], tab_words[0].rearrange("p t i -> p (t i)").bitcast(I32))
+        pos1_t = load_list("pos1_t", pos1)
+        pos2_t = load_list("pos2_t", pos2)
+        pos3_t = load_list("pos3_t", pos3)
+        pos4_t = load_list("pos4_t", pos4)
+        gain_t = keep.tile([P, SLICES], F32, name="gain_t")
+        nc.sync.dma_start(
+            gain_t[:].rearrange("p (b t) -> p b t", t=PACK), gain.rearrange("(b p t) -> p b t", p=P, t=PACK)
+        )
+        pos5_t = load_list("pos5_t", pos5)
+        pos6_t = load_list("pos6_t", pos6)
+        load_w1(2)
+        load_w1(3)
+        wrec_raw = []
+        for b in range(R_PASSES):
+            for c in range(N // WREC_CHUNK):
+                raw = keep.tile([P, PACK, WREC_CHUNK], F32, name="wrec_raw%d_%d" % (b, c))
+                rows = wrec[b * K_PASS : (b + 1) * K_PASS, c * WREC_CHUNK : (c + 1) * WREC_CHUNK]
+                nc.sync.dma_start(raw[:], rows.rearrange("(p j) n -> p j n", j=PACK))
+                wrec_raw.append(raw)
+        wsq_codes = keep.tile([P, R_PASSES, 2 * N], U8, name="wsq_codes", align_bytes=64)
+        nc.sync.dma_start(wsq_codes[:].bitcast(I32), wsq_words.rearrange("a p c -> p a c").bitcast(I32))
+        wsq_plane = keep.tile([P, R_PASSES, N], U8, name="wsq_plane", align_bytes=64)
+        nc.vector.memset(wsq_plane[:].bitcast(I32), 0)
+        for q in range(4):
+            nc.sync.dma_start(
+                wsq_plane[32 * q : 32 * q + 4, :, :].bitcast(I32),
+                wsq_scales[:, 4 * q : 4 * q + 4, :].rearrange("a r n -> r a n").bitcast(I32),
+            )
+
+        picked_scales = keep.tile([P, S], U8, name="picked_scales", align_bytes=64)
+        nc.vector.tensor_copy(picked_scales[:], table_scales[:].indirect(offs_t[:]))
+        picked_words = head.tile([P, S], U32, name="picked_words", align_bytes=64, offset=0)
+
+        def pick_words():
+            for c in range(S // BANK):
+                entries = offs_t[:, c * BANK // 16 : (c + 1) * BANK // 16]
+                nc.vector.tensor_copy(
+                    picked_words[:, c * BANK : (c + 1) * BANK], table_words[:].bitcast(U32).indirect(entries)
+                )
+
+        w1_codes = head.tile([P, H], U32, name="w1_codes", align_bytes=64, offset=4 * S)
+        w1_plane = keep.tile([P, H], U8, name="w1_plane", align_bytes=64)
+
+        def quantize_w1(b):
+            grouped = ring.tile([P, PACK, P, PACK], BF16, name="w1_grouped", align_bytes=64)
+            per_chunk = W1_CHUNK // PACK
+            for half in range(K_PASS // W1_CHUNK):
+                nc.scalar.copy(
+                    grouped[:, :, half * per_chunk : (half + 1) * per_chunk, :].rearrange("p t m j -> p m t j"),
+                    w1_raw[2 * b + half][:].rearrange("p j (m t) -> p m t j", t=PACK),
+                )
+            for t in range(PACK):
+                cols = slice((b * PACK + t) * P, (b * PACK + t + 1) * P)
+                nc.vector.quantize_mx(
+                    out=w1_codes[:, cols].bitcast(FP8X4),
+                    scales=w1_plane[:, cols],
+                    in_=grouped[:, t, :, :].rearrange("p m j -> p (m j)"),
+                )
+
+        wrec_codes = keep.tile([P, R_PASSES * N], U32, name="wrec_codes", align_bytes=64)
+        wrec_plane = keep.tile([P, R_PASSES * N], U8, name="wrec_plane", align_bytes=64)
+
+        def quantize_wrec(i):
+            grouped = ring.tile([P, WREC_CHUNK, PACK], BF16, name="wrec_grouped", align_bytes=64)
+            for half in range(2):
+                part = slice(half * WREC_CHUNK // 2, (half + 1) * WREC_CHUNK // 2)
+                nc.scalar.copy(grouped[:, part, :], wrec_raw[i][:, :, part].rearrange("p j n -> p n j"))
+            cols = slice(i * WREC_CHUNK, (i + 1) * WREC_CHUNK)
+            nc.vector.quantize_mx(
+                out=wrec_codes[:, cols].bitcast(FP8X4),
+                scales=wrec_plane[:, cols],
+                in_=grouped[:].rearrange("p n j -> p (n j)"),
+            )
+
+        h, g1, a1, g3, prod, a2 = {}, {}, {}, {}, {}, {}
+        first = [keep.tile([P, PACK, P3], F32, name="first%d" % b) for b in range(R_PASSES)]
+        slide = keep.tile([P, (SLICES - 1) * P3 + P1], F32, name="slide")
+        y = [y_psum.tile([P, P3], F32, name="y%d" % n) for n in range(N_TILES)]
+        last = SLICES - 1
+
+        def second(s):
+            return slide[:, s * P3 : s * P3 + P1]
+
+        def features(s):
+            h[s] = slots.tile([P, S], F32, name="h%d" % s, offset=(s % H_SLOTS) * S * 4)
+            rows = slice(s * P, (s + 1) * P)
+            for c in range(S // BANK):
+                cols = slice(c * BANK, (c + 1) * BANK)
+                acc = h_psum.tile([P, BANK], F32, name="acc")
+                nc.tensor.matmul_mx(
+                    out=acc[:],
+                    lhsT=w1_codes[:, rows].bitcast(FP8X4),
+                    lhsT_scale=w1_plane[:, rows],
+                    rhs=picked_words[:, cols].bitcast(FP8X4),
+                    rhs_scale=picked_scales[:, cols],
+                    start=True,
+                    stop=True,
+                )
+                nc.scalar.activation(h[s][:, cols], acc[:], ACT.Tanh)
+
+        def pick_pos1(s):
+            g1[s] = slots.tile([P, P1], F32, name="g1_%d" % s, offset=((s - 1) % H_SLOTS) * S * 4)
+            nc.vector.tensor_copy(g1[s][:], h[s][:].indirect(pos1_t[:]))
+
+        def pick_pos2(s):
+            if s >= 0:
+                nc.vector.tensor_copy(second(s), h[s][:].indirect(pos2_t[:]))
+            else:
+                nc.vector.tensor_tensor(second(s), h[s][:].indirect(pos2_t[:]), g1[s][:], ALU.subtract)
+                nc.scalar.activation(second(s), second(s), ACT.Relu)
+
+        def larger(s):
+            a1[s] = ring.tile([P, P1], F32, name="a1", bufs=2)
+            if s >= 0:
+                nc.vector.tensor_tensor(a1[s][:], g1[s][:], second(s), ALU.max)
+            else:
+                nc.gpsimd.tensor_tensor(a1[s][:], g1[s][:], second(s), ALU.add)
+
+        def pick_pos3(s):
+            g3[s] = ring.tile([P, P2], F32, name="g3")
+            nc.vector.tensor_copy(g3[s][:], a1[s][:].indirect(pos3_t[:]))
+
+        def product(s):
+            prod[s] = ring.tile([P, P2], F32, name="prod")
+            nc.vector.tensor_tensor(prod[s][:], a1[s][:].indirect(pos4_t[:]), g3[s][:], ALU.mult)
+            a2[s] = ring.tile([P, P2], F32, name="a2")
+            if s == last:
+                nc.vector.tensor_scalar(a2[s][:], prod[s][:], gain_t[:, s : s + 1], None, ALU.mult)
+            else:
+                nc.scalar.activation(a2[s][:], prod[s][:], ACT.Copy, scale=gain_t[:, s : s + 1])
+
+        def pick_pos5(s):
+            b, t = divmod(s, PACK)
+            nc.vector.tensor_copy(first[b][:, t, :], a2[s][:].indirect(pos5_t[:]))
+
+        def difference(s):
+            b, t = divmod(s, PACK)
+            diff = slide[:, (s + 1) * P3 : (s + 2) * P3]
+            nc.vector.tensor_tensor(diff, a2[s][:].indirect(pos6_t[:]), first[b][:, t, :], ALU.subtract)
+
+        def quantize_level3(name, grouped):
+            codes = ring.tile([P, P3], U32, name=name + "_codes", align_bytes=64)
+            plane = ring.tile([P, P3], U8, name=name + "_plane", align_bytes=64)
+            nc.vector.quantize_mx(
+                out=codes[:].bitcast(FP8X4), scales=plane[:], in_=grouped[:].rearrange("p c t -> p (c t)")
+            )
+            return codes, plane
+
+        def second_stage(b):
+            diffs = slide[:, (b * PACK + 1) * P3 : (b * PACK + PACK + 1) * P3]
+            a3_grouped = ring.tile([P, P3, PACK], BF16, name="a3_grouped", align_bytes=64)
+            nc.scalar.activation(a3_grouped[:], diffs.rearrange("p (t c) -> p c t", t=PACK), ACT.Abs)
+            first_grouped = ring.tile([P, P3, PACK], BF16, name="first_grouped", align_bytes=64)
+            if b == R_PASSES - 1:
+                nc.vector.tensor_copy(first_grouped[:], first[b][:].rearrange("p t c -> p c t"))
+            else:
+                nc.scalar.copy(first_grouped[:], first[b][:].rearrange("p t c -> p c t"))
+            first_codes, first_plane = quantize_level3("first", first_grouped)
+            a3_codes, a3_plane = quantize_level3("a3", a3_grouped)
+            for n in range(N_TILES):
+                cols = slice(b * N + n * P, b * N + (n + 1) * P)
+                nc.tensor.matmul_mx(
+                    out=y[n][:],
+                    lhsT=wrec_codes[:, cols].bitcast(FP8X4),
+                    lhsT_scale=wrec_plane[:, cols],
+                    rhs=first_codes[:].bitcast(FP8X4),
+                    rhs_scale=first_plane[:],
+                    start=(b == 0),
+                    stop=False,
+                )
+            for n in range(N_TILES):
+                nc.tensor.matmul_mx(
+                    out=y[n][:],
+                    lhsT=wsq_codes[:, b, 2 * n * P : 2 * (n + 1) * P].bitcast(FP4X4),
+                    lhsT_scale=wsq_plane[:, b, n * P : (n + 1) * P],
+                    rhs=a3_codes[:].bitcast(FP8X4),
+                    rhs_scale=a3_plane[:],
+                    start=False,
+                    stop=(b == R_PASSES - 1),
+                )
+
+        quantize_w1(0)
+        pick_words()
+        features(0)
+        features(1)
+        for i in range(-1, SLICES + 1):
+            if i + 1 < SLICES:
+                pick_pos1(i + 1)
+            if i - 1 >= 0:
+                pick_pos5(i - 1)
+            if 0 <= i < SLICES:
+                pick_pos3(i)
+            if i + 1 < SLICES:
+                pick_pos2(i + 1)
+            if i - 1 >= 0:
+                difference(i - 1)
+            if 0 <= i < SLICES:
+                product(i)
+            if i + 1 < SLICES:
+                larger(i + 1)
+            if i == -1:
+                quantize_w1(1)
+            if i + 3 < SLICES:
+                features(i + 3)
+            if i - 1 >= 0 and (i - 1) % PACK == PACK - 1:
+                second_stage((i - 1) // PACK)
+            if 0 <= i < len(wrec_raw):
+                quantize_wrec(i)
+
+        for n in range(N_TILES):
+            result = ring.tile([P, P3], F32, name="result", bufs=N_TILES)
+            nc.scalar.activation(result[:], y[n][:], ACT.Tanh)
+            nc.sync.dma_start(out[n * P : (n + 1) * P, :], result[:])

@@ -169,15 +169,15 @@ def tile_list_academy_squad_trials_kernel(
             nc.vector.tensor_copy(g1[s][:], h[s][:].indirect(pos1_t[:]))
 
         def pick_pos2(s):
-            if s >= 0:
+            if s == last:
                 nc.vector.tensor_copy(second(s), h[s][:].indirect(pos2_t[:]))
             else:
                 nc.vector.tensor_tensor(second(s), h[s][:].indirect(pos2_t[:]), g1[s][:], ALU.subtract)
                 nc.scalar.activation(second(s), second(s), ACT.Relu)
 
         def larger(s):
-            a1[s] = ring.tile([P, P1], F32, name="a1", bufs=2)
-            if s >= 0:
+            a1[s] = ring.tile([P, P1], F32, name="a1", bufs=1)
+            if s == last:
                 nc.vector.tensor_tensor(a1[s][:], g1[s][:], second(s), ALU.max)
             else:
                 nc.gpsimd.tensor_tensor(a1[s][:], g1[s][:], second(s), ALU.add)

@@ -25,7 +25,8 @@ SLICES = R_PASSES * PACK
 N_TILES = N // P
 W1_CHUNK = 256
 WREC_CHUNK = 384
-H_SLOTS = 3
+WREC_COPY = 128
+WREC_SPLIT = 1024
 
 
 def tile_list_academy_squad_trials_kernel(
@@ -36,8 +37,6 @@ def tile_list_academy_squad_trials_kernel(
         lists = ctx.enter_context(tc.tile_pool(name="lists", bufs=1))
         keep = ctx.enter_context(tc.tile_pool(name="keep", bufs=1))
         ring = ctx.enter_context(tc.tile_pool(name="ring", bufs=2))
-        slots = ctx.enter_context(tc.tile_pool(name="slots", bufs=1))
-        head = ctx.enter_context(tc.tile_pool(name="head", bufs=1))
         h_psum = ctx.enter_context(tc.psum_pool(name="h_psum", bufs=2))
         y_psum = ctx.enter_context(tc.psum_pool(name="y_psum", bufs=1))
 
@@ -46,36 +45,30 @@ def tile_list_academy_squad_trials_kernel(
             nc.sync.dma_start(t[:], src)
             return t
 
-        table_scales = head.tile([P, T], U8, name="table_scales", align_bytes=64, offset=4 * S - T // 2)
+        table_scales = keep.tile([P, T], U8, name="table_scales", align_bytes=64)
         nc.vector.memset(table_scales[:].bitcast(I32), 0)
         offs_t = load_list("offs_t", offs)
         for q in range(4):
-            nc.scalar.dma_start(
+            nc.sync.dma_start(
                 table_scales[32 * q : 32 * q + 4, :].bitcast(I32), tab_scales[0, 4 * q : 4 * q + 4, :].bitcast(I32)
             )
-        w1_raw = []
-
-        def load_w1(c):
-            raw = keep.tile([P, PACK, W1_CHUNK], F32, name="w1_raw%d" % c)
-            nc.sync.dma_start(raw[:], w1[:, c * W1_CHUNK : (c + 1) * W1_CHUNK].rearrange("(p j) c -> p j c", j=PACK))
-            w1_raw.append(raw)
-
-        load_w1(0)
-        load_w1(1)
-        table_words = keep.tile([P, T], I32, name="table_words", align_bytes=64)
-        nc.sync.dma_start(table_words[:], tab_words[0].rearrange("p t i -> p (t i)").bitcast(I32))
         pos1_t = load_list("pos1_t", pos1)
         pos2_t = load_list("pos2_t", pos2)
         pos3_t = load_list("pos3_t", pos3)
         pos4_t = load_list("pos4_t", pos4)
+        pos5_t = load_list("pos5_t", pos5)
+        pos6_t = load_list("pos6_t", pos6)
         gain_t = keep.tile([P, SLICES], F32, name="gain_t")
         nc.sync.dma_start(
             gain_t[:].rearrange("p (b t) -> p b t", t=PACK), gain.rearrange("(b p t) -> p b t", p=P, t=PACK)
         )
-        pos5_t = load_list("pos5_t", pos5)
-        pos6_t = load_list("pos6_t", pos6)
-        load_w1(2)
-        load_w1(3)
+        table_words = keep.tile([P, T], I32, name="table_words", align_bytes=64)
+        nc.sync.dma_start(table_words[:], tab_words[0].rearrange("p t i -> p (t i)").bitcast(I32))
+        w1_raw = []
+        for c in range(H // W1_CHUNK):
+            raw = keep.tile([P, PACK, W1_CHUNK], F32, name="w1_raw%d" % c)
+            nc.sync.dma_start(raw[:], w1[:, c * W1_CHUNK : (c + 1) * W1_CHUNK].rearrange("(p j) c -> p j c", j=PACK))
+            w1_raw.append(raw)
         wrec_raw = []
         for b in range(R_PASSES):
             for c in range(N // WREC_CHUNK):
@@ -93,62 +86,66 @@ def tile_list_academy_squad_trials_kernel(
                 wsq_scales[:, 4 * q : 4 * q + 4, :].rearrange("a r n -> r a n").bitcast(I32),
             )
 
+        def quantize(codes, plane, grouped):
+            nc.vector.quantize_mx(out=codes.bitcast(FP8X4), scales=plane, in_=grouped)
+
         picked_scales = keep.tile([P, S], U8, name="picked_scales", align_bytes=64)
         nc.vector.tensor_copy(picked_scales[:], table_scales[:].indirect(offs_t[:]))
-        picked_words = head.tile([P, S], U32, name="picked_words", align_bytes=64, offset=0)
 
-        def pick_words():
-            for c in range(S // BANK):
-                entries = offs_t[:, c * BANK // 16 : (c + 1) * BANK // 16]
-                nc.vector.tensor_copy(
-                    picked_words[:, c * BANK : (c + 1) * BANK], table_words[:].bitcast(U32).indirect(entries)
-                )
-
-        w1_codes = head.tile([P, H], U32, name="w1_codes", align_bytes=64, offset=4 * S)
+        w1_codes = keep.tile([P, H], U32, name="w1_codes", align_bytes=64)
         w1_plane = keep.tile([P, H], U8, name="w1_plane", align_bytes=64)
+        per_chunk = W1_CHUNK // PACK
 
-        def quantize_w1(b):
-            grouped = ring.tile([P, PACK, P, PACK], BF16, name="w1_grouped", align_bytes=64)
-            per_chunk = W1_CHUNK // PACK
+        def round_w1(grouped, b, t0, t1):
             for half in range(K_PASS // W1_CHUNK):
+                src = w1_raw[2 * b + half][:].rearrange("p j (m t) -> p m t j", t=PACK)
                 nc.scalar.copy(
                     grouped[:, :, half * per_chunk : (half + 1) * per_chunk, :].rearrange("p t m j -> p m t j"),
-                    w1_raw[2 * b + half][:].rearrange("p j (m t) -> p m t j", t=PACK),
-                )
-            for t in range(PACK):
-                cols = slice((b * PACK + t) * P, (b * PACK + t + 1) * P)
-                nc.vector.quantize_mx(
-                    out=w1_codes[:, cols].bitcast(FP8X4),
-                    scales=w1_plane[:, cols],
-                    in_=grouped[:, t, :, :].rearrange("p m j -> p (m j)"),
+                    src[:, :, t0:t1, :],
                 )
 
+        def quantize_w1(grouped, s0, s1):
+            cols = slice(s0 * P, s1 * P)
+            quantize(w1_codes[:, cols], w1_plane[:, cols], grouped[:].rearrange("p t m j -> p (t m j)"))
+
+        w1_lead = keep.tile([P, 1, P, PACK], BF16, name="w1_lead", tag="lead_then_words", align_bytes=64)
+        round_w1(w1_lead, 0, 0, 1)
+        quantize_w1(w1_lead, 0, 1)
+        picked_words = []
+        for c in range(S // BANK):
+            tag = "lead_then_words" if c == S // BANK - 1 else "words%d" % c
+            words = keep.tile([P, BANK], U32, name="picked_words%d" % c, tag=tag, align_bytes=64)
+            entries = offs_t[:, c * BANK // 16 : (c + 1) * BANK // 16]
+            nc.vector.tensor_copy(words[:], table_words[:].bitcast(U32).indirect(entries))
+            picked_words.append(words)
+
+        wrec_grouped = keep.tile([P, R_PASSES * N, PACK], BF16, name="wrec_grouped", align_bytes=64)
         wrec_codes = keep.tile([P, R_PASSES * N], U32, name="wrec_codes", align_bytes=64)
         wrec_plane = keep.tile([P, R_PASSES * N], U8, name="wrec_plane", align_bytes=64)
 
-        def quantize_wrec(i):
-            grouped = ring.tile([P, WREC_CHUNK, PACK], BF16, name="wrec_grouped", align_bytes=64)
-            for half in range(2):
-                part = slice(half * WREC_CHUNK // 2, (half + 1) * WREC_CHUNK // 2)
-                nc.scalar.copy(grouped[:, part, :], wrec_raw[i][:, :, part].rearrange("p j n -> p n j"))
-            cols = slice(i * WREC_CHUNK, (i + 1) * WREC_CHUNK)
-            nc.vector.quantize_mx(
-                out=wrec_codes[:, cols].bitcast(FP8X4),
-                scales=wrec_plane[:, cols],
-                in_=grouped[:].rearrange("p n j -> p (n j)"),
+        def quantize_wrec(c0, c1):
+            for c in range(c0, c1, WREC_COPY):
+                i, at = divmod(c, WREC_CHUNK)
+                nc.scalar.copy(
+                    wrec_grouped[:, c : c + WREC_COPY, :],
+                    wrec_raw[i][:, :, at : at + WREC_COPY].rearrange("p j n -> p n j"),
+                )
+            quantize(
+                wrec_codes[:, c0:c1], wrec_plane[:, c0:c1], wrec_grouped[:, c0:c1, :].rearrange("p n j -> p (n j)")
             )
 
-        h, g1, a1, g3, prod, a2 = {}, {}, {}, {}, {}, {}
-        first = [keep.tile([P, PACK, P3], F32, name="first%d" % b) for b in range(R_PASSES)]
-        slide = keep.tile([P, (SLICES - 1) * P3 + P1], F32, name="slide")
+        h, a1, a2 = {}, {}, {}
+        step = 2 * P3
+        slide = keep.tile([P, 2, (SLICES // 2) * step + P1], F32, name="slide")
         y = [y_psum.tile([P, P3], F32, name="y%d" % n) for n in range(N_TILES)]
         last = SLICES - 1
 
-        def second(s):
-            return slide[:, s * P3 : s * P3 + P1]
+        def room(s, lo, hi):
+            at = ((s - 1) // 2 + 1) * step
+            return slide[:, (s - 1) % 2, at + lo : at + hi]
 
         def features(s):
-            h[s] = slots.tile([P, S], F32, name="h%d" % s, offset=(s % H_SLOTS) * S * 4)
+            h[s] = ring.tile([P, S], F32, name="h", bufs=3)
             rows = slice(s * P, (s + 1) * P)
             for c in range(S // BANK):
                 cols = slice(c * BANK, (c + 1) * BANK)
@@ -157,80 +154,80 @@ def tile_list_academy_squad_trials_kernel(
                     out=acc[:],
                     lhsT=w1_codes[:, rows].bitcast(FP8X4),
                     lhsT_scale=w1_plane[:, rows],
-                    rhs=picked_words[:, cols].bitcast(FP8X4),
+                    rhs=picked_words[c][:].bitcast(FP8X4),
                     rhs_scale=picked_scales[:, cols],
                     start=True,
                     stop=True,
                 )
                 nc.scalar.activation(h[s][:, cols], acc[:], ACT.Tanh)
 
-        def pick_pos1(s):
-            g1[s] = slots.tile([P, P1], F32, name="g1_%d" % s, offset=((s - 1) % H_SLOTS) * S * 4)
-            nc.vector.tensor_copy(g1[s][:], h[s][:].indirect(pos1_t[:]))
+        excess = {}
 
-        def pick_pos2(s):
-            if s == last:
-                nc.vector.tensor_copy(second(s), h[s][:].indirect(pos2_t[:]))
-            else:
-                nc.vector.tensor_tensor(second(s), h[s][:].indirect(pos2_t[:]), g1[s][:], ALU.subtract)
-                nc.scalar.activation(second(s), second(s), ACT.Relu)
+        def pick_drills(s):
+            g1 = room(s, 0, P1)
+            nc.vector.tensor_copy(g1, h[s][:].indirect(pos1_t[:]))
+            a1[s] = ring.tile([P, P1], F32, name="a1")
+            nc.vector.tensor_copy(a1[s][:], h[s][:].indirect(pos2_t[:]))
+            if s not in (0, last):
+                excess[s] = ring.tile([P, P1], F32, name="excess", bufs=1)
+                nc.gpsimd.tensor_tensor(excess[s][:], a1[s][:], g1, ALU.subtract)
+                nc.scalar.activation(excess[s][:], excess[s][:], ACT.Relu)
 
         def larger(s):
-            a1[s] = ring.tile([P, P1], F32, name="a1", bufs=1)
-            if s == last:
-                nc.vector.tensor_tensor(a1[s][:], g1[s][:], second(s), ALU.max)
+            g1 = room(s, 0, P1)
+            if s in (0, last):
+                nc.vector.tensor_tensor(a1[s][:], g1, a1[s][:], ALU.max)
             else:
-                nc.gpsimd.tensor_tensor(a1[s][:], g1[s][:], second(s), ALU.add)
+                nc.gpsimd.tensor_tensor(a1[s][:], g1, excess[s][:], ALU.add)
 
-        def pick_pos3(s):
-            g3[s] = ring.tile([P, P2], F32, name="g3")
-            nc.vector.tensor_copy(g3[s][:], a1[s][:].indirect(pos3_t[:]))
-
-        def product(s):
-            prod[s] = ring.tile([P, P2], F32, name="prod")
-            nc.vector.tensor_tensor(prod[s][:], a1[s][:].indirect(pos4_t[:]), g3[s][:], ALU.mult)
+        def recruits(s):
+            g3 = ring.tile([P, P2], F32, name="g3")
+            nc.vector.tensor_copy(g3[:], a1[s][:].indirect(pos3_t[:]))
+            g4 = ring.tile([P, P2], F32, name="g4")
             a2[s] = ring.tile([P, P2], F32, name="a2")
-            if s == last:
-                nc.vector.tensor_scalar(a2[s][:], prod[s][:], gain_t[:, s : s + 1], None, ALU.mult)
+            if s >= last - 1:
+                nc.vector.tensor_tensor(g4[:], a1[s][:].indirect(pos4_t[:]), g3[:], ALU.mult)
+                if s == last:
+                    nc.vector.tensor_scalar(a2[s][:], g4[:], gain_t[:, s : s + 1], None, ALU.mult)
+                else:
+                    nc.scalar.activation(a2[s][:], g4[:], ACT.Copy, scale=gain_t[:, s : s + 1])
             else:
-                nc.scalar.activation(a2[s][:], prod[s][:], ACT.Copy, scale=gain_t[:, s : s + 1])
+                nc.vector.tensor_copy(g4[:], a1[s][:].indirect(pos4_t[:]))
+                nc.scalar.activation(g3[:], g3[:], ACT.Copy, scale=gain_t[:, s : s + 1])
+                nc.gpsimd.tensor_tensor(a2[s][:], g4[:], g3[:], ALU.mult)
 
-        def pick_pos5(s):
-            b, t = divmod(s, PACK)
-            nc.vector.tensor_copy(first[b][:, t, :], a2[s][:].indirect(pos5_t[:]))
-
-        def difference(s):
-            b, t = divmod(s, PACK)
-            diff = slide[:, (s + 1) * P3 : (s + 2) * P3]
-            nc.vector.tensor_tensor(diff, a2[s][:].indirect(pos6_t[:]), first[b][:, t, :], ALU.subtract)
-
-        def quantize_level3(name, grouped):
-            codes = ring.tile([P, P3], U32, name=name + "_codes", align_bytes=64)
-            plane = ring.tile([P, P3], U8, name=name + "_plane", align_bytes=64)
-            nc.vector.quantize_mx(
-                out=codes[:].bitcast(FP8X4), scales=plane[:], in_=grouped[:].rearrange("p c t -> p (c t)")
-            )
-            return codes, plane
+        def squads(s):
+            first, diff = room(s + 1, 0, P3), room(s + 1, P3, 2 * P3)
+            nc.vector.tensor_copy(first, a2[s][:].indirect(pos5_t[:]))
+            if s >= last - 2:
+                nc.vector.tensor_tensor(diff, a2[s][:].indirect(pos6_t[:]), first, ALU.subtract)
+            else:
+                nc.vector.tensor_copy(diff, a2[s][:].indirect(pos6_t[:]))
+                nc.gpsimd.tensor_tensor(diff, diff, first, ALU.subtract)
 
         def second_stage(b):
-            diffs = slide[:, (b * PACK + 1) * P3 : (b * PACK + PACK + 1) * P3]
-            a3_grouped = ring.tile([P, P3, PACK], BF16, name="a3_grouped", align_bytes=64)
-            nc.scalar.activation(a3_grouped[:], diffs.rearrange("p (t c) -> p c t", t=PACK), ACT.Abs)
-            first_grouped = ring.tile([P, P3, PACK], BF16, name="first_grouped", align_bytes=64)
+            both = slide[:, :, (2 * b + 1) * step : (2 * b + 3) * step].rearrange("p v (u k c) -> p k c u v", u=2, k=2)
+            grouped = ring.tile([P, 2, P3, PACK], BF16, name="level3_grouped", align_bytes=64)
+            codes = ring.tile([P, 2 * P3], U32, name="level3_codes", align_bytes=64)
+            plane = ring.tile([P, 2 * P3], U8, name="level3_plane", align_bytes=64)
+            dst = grouped[:].rearrange("p k c (u v) -> p k c u v", u=2)
+            nc.scalar.activation(dst[:, 1, :, :, :], both[:, 1, :, :, :], ACT.Abs)
             if b == R_PASSES - 1:
-                nc.vector.tensor_copy(first_grouped[:], first[b][:].rearrange("p t c -> p c t"))
+                nc.vector.tensor_copy(dst[:, 0, :, :, :], both[:, 0, :, :, :])
+                for k in range(2):
+                    cols = slice(k * P3, (k + 1) * P3)
+                    quantize(codes[:, cols], plane[:, cols], grouped[:, k, :, :].rearrange("p c t -> p (c t)"))
             else:
-                nc.scalar.copy(first_grouped[:], first[b][:].rearrange("p t c -> p c t"))
-            first_codes, first_plane = quantize_level3("first", first_grouped)
-            a3_codes, a3_plane = quantize_level3("a3", a3_grouped)
+                nc.scalar.copy(dst[:, 0, :, :, :], both[:, 0, :, :, :])
+                quantize(codes[:], plane[:], grouped[:].rearrange("p k c t -> p (k c t)"))
             for n in range(N_TILES):
                 cols = slice(b * N + n * P, b * N + (n + 1) * P)
                 nc.tensor.matmul_mx(
                     out=y[n][:],
                     lhsT=wrec_codes[:, cols].bitcast(FP8X4),
                     lhsT_scale=wrec_plane[:, cols],
-                    rhs=first_codes[:].bitcast(FP8X4),
-                    rhs_scale=first_plane[:],
+                    rhs=codes[:, 0:P3].bitcast(FP8X4),
+                    rhs_scale=plane[:, 0:P3],
                     start=(b == 0),
                     stop=False,
                 )
@@ -239,39 +236,38 @@ def tile_list_academy_squad_trials_kernel(
                     out=y[n][:],
                     lhsT=wsq_codes[:, b, 2 * n * P : 2 * (n + 1) * P].bitcast(FP4X4),
                     lhsT_scale=wsq_plane[:, b, n * P : (n + 1) * P],
-                    rhs=a3_codes[:].bitcast(FP8X4),
-                    rhs_scale=a3_plane[:],
+                    rhs=codes[:, P3 : 2 * P3].bitcast(FP8X4),
+                    rhs_scale=plane[:, P3 : 2 * P3],
                     start=False,
                     stop=(b == R_PASSES - 1),
                 )
 
-        quantize_w1(0)
-        pick_words()
         features(0)
+        w1_rest = keep.tile([P, PACK - 1, P, PACK], BF16, name="w1_rest", align_bytes=64)
+        round_w1(w1_rest, 0, 1, PACK)
+        quantize_w1(w1_rest, 1, PACK)
         features(1)
-        for i in range(-1, SLICES + 1):
-            if i + 1 < SLICES:
-                pick_pos1(i + 1)
-            if i - 1 >= 0:
-                pick_pos5(i - 1)
-            if 0 <= i < SLICES:
-                pick_pos3(i)
-            if i + 1 < SLICES:
-                pick_pos2(i + 1)
-            if i - 1 >= 0:
-                difference(i - 1)
-            if 0 <= i < SLICES:
-                product(i)
-            if i + 1 < SLICES:
-                larger(i + 1)
-            if i == -1:
-                quantize_w1(1)
-            if i + 3 < SLICES:
-                features(i + 3)
-            if i - 1 >= 0 and (i - 1) % PACK == PACK - 1:
-                second_stage((i - 1) // PACK)
-            if 0 <= i < len(wrec_raw):
-                quantize_wrec(i)
+        for i in range(SLICES + 2):
+            if i < SLICES:
+                pick_drills(i)
+            if 0 <= i - 1 < SLICES:
+                recruits(i - 1)
+            if i < SLICES:
+                larger(i)
+            if 0 <= i - 2:
+                squads(i - 2)
+            if i + 2 < SLICES:
+                features(i + 2)
+            if i == 0:
+                w1_second = keep.tile([P, PACK, P, PACK], BF16, name="w1_second", align_bytes=64)
+                round_w1(w1_second, 1, 0, PACK)
+                quantize_w1(w1_second, PACK, 2 * PACK)
+            if i == 1:
+                quantize_wrec(0, WREC_SPLIT)
+            if i == 2:
+                quantize_wrec(WREC_SPLIT, R_PASSES * N)
+            if i - 2 >= 0 and (i - 2) % PACK == PACK - 1:
+                second_stage((i - 2) // PACK)
 
         for n in range(N_TILES):
             result = ring.tile([P, P3], F32, name="result", bufs=N_TILES)

@@ -27,6 +27,7 @@ W1_CHUNK = 256
 WREC_CHUNK = 384
 WREC_COPY = 128
 WREC_SPLIT = 1024
+H_SLOTS = 3
 
 
 def tile_list_academy_squad_trials_kernel(
@@ -37,6 +38,7 @@ def tile_list_academy_squad_trials_kernel(
         lists = ctx.enter_context(tc.tile_pool(name="lists", bufs=1))
         keep = ctx.enter_context(tc.tile_pool(name="keep", bufs=1))
         ring = ctx.enter_context(tc.tile_pool(name="ring", bufs=2))
+        slots = ctx.enter_context(tc.tile_pool(name="slots", bufs=1))
         h_psum = ctx.enter_context(tc.psum_pool(name="h_psum", bufs=2))
         y_psum = ctx.enter_context(tc.psum_pool(name="y_psum", bufs=1))
 
@@ -52,23 +54,28 @@ def tile_list_academy_squad_trials_kernel(
             nc.sync.dma_start(
                 table_scales[32 * q : 32 * q + 4, :].bitcast(I32), tab_scales[0, 4 * q : 4 * q + 4, :].bitcast(I32)
             )
+        w1_raw = []
+
+        def load_w1(c):
+            raw = keep.tile([P, PACK, W1_CHUNK], F32, name="w1_raw%d" % c)
+            nc.sync.dma_start(raw[:], w1[:, c * W1_CHUNK : (c + 1) * W1_CHUNK].rearrange("(p j) c -> p j c", j=PACK))
+            w1_raw.append(raw)
+
+        load_w1(0)
         pos1_t = load_list("pos1_t", pos1)
         pos2_t = load_list("pos2_t", pos2)
+        table_words = keep.tile([P, T], I32, name="table_words", align_bytes=64)
+        nc.sync.dma_start(table_words[:], tab_words[0].rearrange("p t i -> p (t i)").bitcast(I32))
+        for c in range(1, H // W1_CHUNK):
+            load_w1(c)
         pos3_t = load_list("pos3_t", pos3)
         pos4_t = load_list("pos4_t", pos4)
-        pos5_t = load_list("pos5_t", pos5)
-        pos6_t = load_list("pos6_t", pos6)
         gain_t = keep.tile([P, SLICES], F32, name="gain_t")
         nc.sync.dma_start(
             gain_t[:].rearrange("p (b t) -> p b t", t=PACK), gain.rearrange("(b p t) -> p b t", p=P, t=PACK)
         )
-        table_words = keep.tile([P, T], I32, name="table_words", align_bytes=64)
-        nc.sync.dma_start(table_words[:], tab_words[0].rearrange("p t i -> p (t i)").bitcast(I32))
-        w1_raw = []
-        for c in range(H // W1_CHUNK):
-            raw = keep.tile([P, PACK, W1_CHUNK], F32, name="w1_raw%d" % c)
-            nc.sync.dma_start(raw[:], w1[:, c * W1_CHUNK : (c + 1) * W1_CHUNK].rearrange("(p j) c -> p j c", j=PACK))
-            w1_raw.append(raw)
+        pos5_t = load_list("pos5_t", pos5)
+        pos6_t = load_list("pos6_t", pos6)
         wrec_raw = []
         for b in range(R_PASSES):
             for c in range(N // WREC_CHUNK):
@@ -111,12 +118,14 @@ def tile_list_academy_squad_trials_kernel(
         w1_lead = keep.tile([P, 1, P, PACK], BF16, name="w1_lead", tag="lead_then_words", align_bytes=64)
         round_w1(w1_lead, 0, 0, 1)
         quantize_w1(w1_lead, 0, 1)
+        words_early = keep.tile([P, S // 2], U32, name="words_early", align_bytes=64)
+        words_late = keep.tile([P, S // 2], U32, name="words_late", tag="lead_then_words", align_bytes=64)
         picked_words = []
         for c in range(S // BANK):
-            tag = "lead_then_words" if c == S // BANK - 1 else "words%d" % c
-            words = keep.tile([P, BANK], U32, name="picked_words%d" % c, tag=tag, align_bytes=64)
+            half, at = divmod(c * BANK, S // 2)
+            words = (words_early, words_late)[half][:, at : at + BANK]
             entries = offs_t[:, c * BANK // 16 : (c + 1) * BANK // 16]
-            nc.vector.tensor_copy(words[:], table_words[:].bitcast(U32).indirect(entries))
+            nc.vector.tensor_copy(words, table_words[:].bitcast(U32).indirect(entries))
             picked_words.append(words)
 
         wrec_grouped = keep.tile([P, R_PASSES * N, PACK], BF16, name="wrec_grouped", align_bytes=64)
@@ -144,8 +153,11 @@ def tile_list_academy_squad_trials_kernel(
             at = ((s - 1) // 2 + 1) * step
             return slide[:, (s - 1) % 2, at + lo : at + hi]
 
+        def a1_offset(s):
+            return H_SLOTS * S * 4 + (s % 2) * P1 * 4
+
         def features(s):
-            h[s] = ring.tile([P, S], F32, name="h", bufs=3)
+            h[s] = slots.tile([P, S], F32, name="h%d" % s, offset=(s % H_SLOTS) * S * 4)
             rows = slice(s * P, (s + 1) * P)
             for c in range(S // BANK):
                 cols = slice(c * BANK, (c + 1) * BANK)
@@ -154,7 +166,7 @@ def tile_list_academy_squad_trials_kernel(
                     out=acc[:],
                     lhsT=w1_codes[:, rows].bitcast(FP8X4),
                     lhsT_scale=w1_plane[:, rows],
-                    rhs=picked_words[c][:].bitcast(FP8X4),
+                    rhs=picked_words[c].bitcast(FP8X4),
                     rhs_scale=picked_scales[:, cols],
                     start=True,
                     stop=True,
@@ -166,7 +178,7 @@ def tile_list_academy_squad_trials_kernel(
         def pick_drills(s):
             g1 = room(s, 0, P1)
             nc.vector.tensor_copy(g1, h[s][:].indirect(pos1_t[:]))
-            a1[s] = ring.tile([P, P1], F32, name="a1")
+            a1[s] = slots.tile([P, P1], F32, name="a1_%d" % s, offset=a1_offset(s))
             nc.vector.tensor_copy(a1[s][:], h[s][:].indirect(pos2_t[:]))
             if s not in (0, last):
                 excess[s] = ring.tile([P, P1], F32, name="excess", bufs=1)
@@ -183,42 +195,43 @@ def tile_list_academy_squad_trials_kernel(
         def recruits(s):
             g3 = ring.tile([P, P2], F32, name="g3")
             nc.vector.tensor_copy(g3[:], a1[s][:].indirect(pos3_t[:]))
-            g4 = ring.tile([P, P2], F32, name="g4")
-            a2[s] = ring.tile([P, P2], F32, name="a2")
-            if s >= last - 1:
-                nc.vector.tensor_tensor(g4[:], a1[s][:].indirect(pos4_t[:]), g3[:], ALU.mult)
-                if s == last:
-                    nc.vector.tensor_scalar(a2[s][:], g4[:], gain_t[:, s : s + 1], None, ALU.mult)
-                else:
-                    nc.scalar.activation(a2[s][:], g4[:], ACT.Copy, scale=gain_t[:, s : s + 1])
-            else:
-                nc.vector.tensor_copy(g4[:], a1[s][:].indirect(pos4_t[:]))
-                nc.scalar.activation(g3[:], g3[:], ACT.Copy, scale=gain_t[:, s : s + 1])
-                nc.gpsimd.tensor_tensor(a2[s][:], g4[:], g3[:], ALU.mult)
+            g4 = slots.tile([P, P2], F32, name="g4_%d" % s, offset=((s + 1) % H_SLOTS) * S * 4)
+            nc.vector.tensor_copy(g4[:], a1[s][:].indirect(pos4_t[:]))
+            nc.scalar.activation(g3[:], g3[:], ACT.Copy, scale=gain_t[:, s : s + 1])
+            a2[s] = ring.tile([P, P2], F32, name="a2", bufs=3)
+            nc.gpsimd.tensor_tensor(a2[s][:], g4[:], g3[:], ALU.mult)
 
         def squads(s):
             first, diff = room(s + 1, 0, P3), room(s + 1, P3, 2 * P3)
             nc.vector.tensor_copy(first, a2[s][:].indirect(pos5_t[:]))
-            if s >= last - 2:
+            if s == last:
                 nc.vector.tensor_tensor(diff, a2[s][:].indirect(pos6_t[:]), first, ALU.subtract)
             else:
                 nc.vector.tensor_copy(diff, a2[s][:].indirect(pos6_t[:]))
                 nc.gpsimd.tensor_tensor(diff, diff, first, ALU.subtract)
 
-        def second_stage(b):
+        level3 = {}
+
+        def round_level3(b):
             both = slide[:, :, (2 * b + 1) * step : (2 * b + 3) * step].rearrange("p v (u k c) -> p k c u v", u=2, k=2)
-            grouped = ring.tile([P, 2, P3, PACK], BF16, name="level3_grouped", align_bytes=64)
-            codes = ring.tile([P, 2 * P3], U32, name="level3_codes", align_bytes=64)
-            plane = ring.tile([P, 2 * P3], U8, name="level3_plane", align_bytes=64)
-            dst = grouped[:].rearrange("p k c (u v) -> p k c u v", u=2)
+            level3[b] = ring.tile([P, 2, P3, PACK], BF16, name="level3_grouped", align_bytes=64)
+            dst = level3[b][:].rearrange("p k c (u v) -> p k c u v", u=2)
             nc.scalar.activation(dst[:, 1, :, :, :], both[:, 1, :, :, :], ACT.Abs)
             if b == R_PASSES - 1:
                 nc.vector.tensor_copy(dst[:, 0, :, :, :], both[:, 0, :, :, :])
+            else:
+                nc.scalar.copy(dst[:, 0, :, :, :], both[:, 0, :, :, :])
+
+        def second_stage(b):
+            grouped = level3[b]
+            plane = ring.tile([P, 2 * P3], U8, name="level3_plane", align_bytes=64)
+            if b == R_PASSES - 1:
+                codes = keep.tile([P, 2 * P3], U32, name="level3_codes", align_bytes=64)
                 for k in range(2):
                     cols = slice(k * P3, (k + 1) * P3)
                     quantize(codes[:, cols], plane[:, cols], grouped[:, k, :, :].rearrange("p c t -> p (c t)"))
             else:
-                nc.scalar.copy(dst[:, 0, :, :, :], both[:, 0, :, :, :])
+                codes = slots.tile([P, 2 * P3], U32, name="early_codes", align_bytes=64, offset=a1_offset(last))
                 quantize(codes[:], plane[:], grouped[:].rearrange("p k c t -> p (k c t)"))
             for n in range(N_TILES):
                 cols = slice(b * N + n * P, b * N + (n + 1) * P)
@@ -247,6 +260,7 @@ def tile_list_academy_squad_trials_kernel(
         round_w1(w1_rest, 0, 1, PACK)
         quantize_w1(w1_rest, 1, PACK)
         features(1)
+        features(2)
         for i in range(SLICES + 2):
             if i < SLICES:
                 pick_drills(i)
@@ -256,18 +270,19 @@ def tile_list_academy_squad_trials_kernel(
                 larger(i)
             if 0 <= i - 2:
                 squads(i - 2)
-            if i + 2 < SLICES:
-                features(i + 2)
-            if i == 0:
+                if (i - 2) % PACK == PACK - 1:
+                    round_level3((i - 2) // PACK)
+            if i == 1:
                 w1_second = keep.tile([P, PACK, P, PACK], BF16, name="w1_second", align_bytes=64)
                 round_w1(w1_second, 1, 0, PACK)
                 quantize_w1(w1_second, PACK, 2 * PACK)
-            if i == 1:
-                quantize_wrec(0, WREC_SPLIT)
-            if i == 2:
-                quantize_wrec(WREC_SPLIT, R_PASSES * N)
-            if i - 2 >= 0 and (i - 2) % PACK == PACK - 1:
-                second_stage((i - 2) // PACK)
+            if i + H_SLOTS < SLICES:
+                features(i + H_SLOTS)
+
+        quantize_wrec(0, WREC_SPLIT)
+        quantize_wrec(WREC_SPLIT, R_PASSES * N)
+        for b in range(R_PASSES):
+            second_stage(b)
 
         for n in range(N_TILES):
             result = ring.tile([P, P3], F32, name="result", bufs=N_TILES)

from contextlib import ExitStack

import concourse.mybir as mybir

K, H, N, T, S, P1, P2, P3 = 512, 1024, 768, 4096, 2048, 1024, 512, 256
FLOPS = 2 * K * H * S + 2 * 2 * H * N * P3

F32 = mybir.dt.float32
BF16 = mybir.dt.bfloat16
I32 = mybir.dt.int32
U32 = mybir.dt.uint32
U16 = mybir.dt.uint16
U8 = mybir.dt.uint8
FP8X4 = mybir.dt.float8_e4m3fn_x4
FP4X4 = mybir.dt.float4_e2m1fn_x4
ALU = mybir.AluOpType
ACT = mybir.ActivationFunctionType

P = 128
PACK = 4
K_PASS = P * PACK
BANK = 512
R_PASSES = H // K_PASS
SLICES = R_PASSES * PACK
N_TILES = N // P
W1_CHUNK = 256
WREC_CHUNK = 384
WREC_COPY = 128
WREC_SPLIT = 1024
H_SLOTS = 3


def tile_list_academy_squad_trials_kernel(
    tc, tab_words, tab_scales, offs, pos1, pos2, pos3, pos4, pos5, pos6, w1, gain, wsq_words, wsq_scales, wrec, out
):
    nc = tc.nc
    with ExitStack() as ctx:
        lists = ctx.enter_context(tc.tile_pool(name="lists", bufs=1))
        keep = ctx.enter_context(tc.tile_pool(name="keep", bufs=1))
        ring = ctx.enter_context(tc.tile_pool(name="ring", bufs=2))
        slots = ctx.enter_context(tc.tile_pool(name="slots", bufs=1))
        h_psum = ctx.enter_context(tc.psum_pool(name="h_psum", bufs=2))
        y_psum = ctx.enter_context(tc.psum_pool(name="y_psum", bufs=1))

        def load_list(name, src):
            t = lists.tile(list(src.shape), U16, name=name)
            nc.sync.dma_start(t[:], src)
            return t

        table_scales = keep.tile([P, T], U8, name="table_scales", align_bytes=64)
        nc.vector.memset(table_scales[:].bitcast(I32), 0)
        offs_t = load_list("offs_t", offs)
        for q in range(4):
            nc.sync.dma_start(
                table_scales[32 * q : 32 * q + 4, :].bitcast(I32), tab_scales[0, 4 * q : 4 * q + 4, :].bitcast(I32)
            )
        w1_raw = []

        def load_w1(c):
            raw = keep.tile([P, PACK, W1_CHUNK], F32, name="w1_raw%d" % c)
            nc.sync.dma_start(raw[:], w1[:, c * W1_CHUNK : (c + 1) * W1_CHUNK].rearrange("(p j) c -> p j c", j=PACK))
            w1_raw.append(raw)

        load_w1(0)
        pos1_t = load_list("pos1_t", pos1)
        pos2_t = load_list("pos2_t", pos2)
        table_words = keep.tile([P, T], I32, name="table_words", align_bytes=64)
        nc.sync.dma_start(table_words[:], tab_words[0].rearrange("p t i -> p (t i)").bitcast(I32))
        for c in range(1, H // W1_CHUNK):
            load_w1(c)
        pos3_t = load_list("pos3_t", pos3)
        pos4_t = load_list("pos4_t", pos4)
        gain_t = keep.tile([P, SLICES], F32, name="gain_t")
        nc.sync.dma_start(
            gain_t[:].rearrange("p (b t) -> p b t", t=PACK), gain.rearrange("(b p t) -> p b t", p=P, t=PACK)
        )
        pos5_t = load_list("pos5_t", pos5)
        pos6_t = load_list("pos6_t", pos6)
        wrec_raw = []
        for b in range(R_PASSES):
            for c in range(N // WREC_CHUNK):
                raw = keep.tile([P, PACK, WREC_CHUNK], F32, name="wrec_raw%d_%d" % (b, c))
                rows = wrec[b * K_PASS : (b + 1) * K_PASS, c * WREC_CHUNK : (c + 1) * WREC_CHUNK]
                nc.sync.dma_start(raw[:], rows.rearrange("(p j) n -> p j n", j=PACK))
                wrec_raw.append(raw)
        wsq_codes = keep.tile([P, R_PASSES, 2 * N], U8, name="wsq_codes", align_bytes=64)
        nc.sync.dma_start(wsq_codes[:].bitcast(I32), wsq_words.rearrange("a p c -> p a c").bitcast(I32))
        wsq_plane = keep.tile([P, R_PASSES, N], U8, name="wsq_plane", align_bytes=64)
        nc.vector.memset(wsq_plane[:].bitcast(I32), 0)
        for q in range(4):
            nc.sync.dma_start(
                wsq_plane[32 * q : 32 * q + 4, :, :].bitcast(I32),
                wsq_scales[:, 4 * q : 4 * q + 4, :].rearrange("a r n -> r a n").bitcast(I32),
            )

        def quantize(codes, plane, grouped):
            nc.vector.quantize_mx(out=codes.bitcast(FP8X4), scales=plane, in_=grouped)

        picked_scales = keep.tile([P, S], U8, name="picked_scales", align_bytes=64)
        nc.vector.tensor_copy(picked_scales[:], table_scales[:].indirect(offs_t[:]))

        w1_codes = keep.tile([P, H], U32, name="w1_codes", align_bytes=64)
        w1_plane = keep.tile([P, H], U8, name="w1_plane", align_bytes=64)
        per_chunk = W1_CHUNK // PACK

        def round_w1(grouped, b, t0, t1):
            for half in range(K_PASS // W1_CHUNK):
                src = w1_raw[2 * b + half][:].rearrange("p j (m t) -> p m t j", t=PACK)
                nc.scalar.copy(
                    grouped[:, :, half * per_chunk : (half + 1) * per_chunk, :].rearrange("p t m j -> p m t j"),
                    src[:, :, t0:t1, :],
                )

        def quantize_w1(grouped, s0, s1):
            cols = slice(s0 * P, s1 * P)
            quantize(w1_codes[:, cols], w1_plane[:, cols], grouped[:].rearrange("p t m j -> p (t m j)"))

        w1_lead = keep.tile([P, 1, P, PACK], BF16, name="w1_lead", tag="lead_then_words", align_bytes=64)
        round_w1(w1_lead, 0, 0, 1)
        quantize_w1(w1_lead, 0, 1)
        words_early = keep.tile([P, S // 2], U32, name="words_early", align_bytes=64)
        words_late = keep.tile([P, S // 2], U32, name="words_late", tag="lead_then_words", align_bytes=64)
        picked_words = []
        for c in range(S // BANK):
            half, at = divmod(c * BANK, S // 2)
            words = (words_early, words_late)[half][:, at : at + BANK]
            entries = offs_t[:, c * BANK // 16 : (c + 1) * BANK // 16]
            nc.vector.tensor_copy(words, table_words[:].bitcast(U32).indirect(entries))
            picked_words.append(words)

        wrec_grouped = keep.tile([P, R_PASSES * N, PACK], BF16, name="wrec_grouped", align_bytes=64)
        wrec_codes = keep.tile([P, R_PASSES * N], U32, name="wrec_codes", align_bytes=64)
        wrec_plane = keep.tile([P, R_PASSES * N], U8, name="wrec_plane", align_bytes=64)

        def quantize_wrec(c0, c1):
            for c in range(c0, c1, WREC_COPY):
                i, at = divmod(c, WREC_CHUNK)
                nc.scalar.copy(
                    wrec_grouped[:, c : c + WREC_COPY, :],
                    wrec_raw[i][:, :, at : at + WREC_COPY].rearrange("p j n -> p n j"),
                )
            quantize(
                wrec_codes[:, c0:c1], wrec_plane[:, c0:c1], wrec_grouped[:, c0:c1, :].rearrange("p n j -> p (n j)")
            )

        h, a1, a2 = {}, {}, {}
        step = 2 * P3
        slide = keep.tile([P, 2, (SLICES // 2) * step + P1], F32, name="slide")
        y = [y_psum.tile([P, P3], F32, name="y%d" % n) for n in range(N_TILES)]
        last = SLICES - 1

        def room(s, lo, hi):
            at = ((s - 1) // 2 + 1) * step
            return slide[:, (s - 1) % 2, at + lo : at + hi]

        def a1_offset(s):
            return H_SLOTS * S * 4 + (s % 2) * P1 * 4

        def features(s):
            h[s] = slots.tile([P, S], F32, name="h%d" % s, offset=(s % H_SLOTS) * S * 4)
            rows = slice(s * P, (s + 1) * P)
            for c in range(S // BANK):
                cols = slice(c * BANK, (c + 1) * BANK)
                acc = h_psum.tile([P, BANK], F32, name="acc")
                nc.tensor.matmul_mx(
                    out=acc[:],
                    lhsT=w1_codes[:, rows].bitcast(FP8X4),
                    lhsT_scale=w1_plane[:, rows],
                    rhs=picked_words[c].bitcast(FP8X4),
                    rhs_scale=picked_scales[:, cols],
                    start=True,
                    stop=True,
                )
                nc.scalar.activation(h[s][:, cols], acc[:], ACT.Tanh)

        excess = {}

        def pick_drills(s):
            g1 = room(s, 0, P1)
            nc.vector.tensor_copy(g1, h[s][:].indirect(pos1_t[:]))
            a1[s] = slots.tile([P, P1], F32, name="a1_%d" % s, offset=a1_offset(s))
            nc.vector.tensor_copy(a1[s][:], h[s][:].indirect(pos2_t[:]))
            if s not in (0, last):
                excess[s] = ring.tile([P, P1], F32, name="excess", bufs=1)
                nc.gpsimd.tensor_tensor(excess[s][:], a1[s][:], g1, ALU.subtract)
                nc.scalar.activation(excess[s][:], excess[s][:], ACT.Relu)

        def larger(s):
            g1 = room(s, 0, P1)
            if s in (0, last):
                nc.vector.tensor_tensor(a1[s][:], g1, a1[s][:], ALU.max)
            else:
                nc.gpsimd.tensor_tensor(a1[s][:], g1, excess[s][:], ALU.add)

        def recruits(s):
            g3 = ring.tile([P, P2], F32, name="g3")
            nc.vector.tensor_copy(g3[:], a1[s][:].indirect(pos3_t[:]))
            g4 = slots.tile([P, P2], F32, name="g4_%d" % s, offset=((s + 1) % H_SLOTS) * S * 4)
            nc.vector.tensor_copy(g4[:], a1[s][:].indirect(pos4_t[:]))
            nc.scalar.activation(g3[:], g3[:], ACT.Copy, scale=gain_t[:, s : s + 1])
            a2[s] = ring.tile([P, P2], F32, name="a2", bufs=3)
            nc.gpsimd.tensor_tensor(a2[s][:], g4[:], g3[:], ALU.mult)

        def squads(s):
            first, diff = room(s + 1, 0, P3), room(s + 1, P3, 2 * P3)
            nc.vector.tensor_copy(first, a2[s][:].indirect(pos5_t[:]))
            if s == last:
                nc.vector.tensor_tensor(diff, a2[s][:].indirect(pos6_t[:]), first, ALU.subtract)
            else:
                nc.vector.tensor_copy(diff, a2[s][:].indirect(pos6_t[:]))
                nc.gpsimd.tensor_tensor(diff, diff, first, ALU.subtract)

        level3 = {}

        def round_level3(b):
            both = slide[:, :, (2 * b + 1) * step : (2 * b + 3) * step].rearrange("p v (u k c) -> p k c u v", u=2, k=2)
            level3[b] = ring.tile([P, 2, P3, PACK], BF16, name="level3_grouped", align_bytes=64)
            dst = level3[b][:].rearrange("p k c (u v) -> p k c u v", u=2)
            nc.scalar.activation(dst[:, 1, :, :, :], both[:, 1, :, :, :], ACT.Abs)
            if b == R_PASSES - 1:
                nc.vector.tensor_copy(dst[:, 0, :, :, :], both[:, 0, :, :, :])
            else:
                nc.scalar.copy(dst[:, 0, :, :, :], both[:, 0, :, :, :])

        def second_stage(b):
            grouped = level3[b]
            plane = ring.tile([P, 2 * P3], U8, name="level3_plane", align_bytes=64)
            if b == R_PASSES - 1:
                codes = keep.tile([P, 2 * P3], U32, name="level3_codes", align_bytes=64)
                for k in range(2):
                    cols = slice(k * P3, (k + 1) * P3)
                    quantize(codes[:, cols], plane[:, cols], grouped[:, k, :, :].rearrange("p c t -> p (c t)"))
            else:
                codes = slots.tile([P, 2 * P3], U32, name="early_codes", align_bytes=64, offset=a1_offset(last))
                quantize(codes[:], plane[:], grouped[:].rearrange("p k c t -> p (k c t)"))
            for n in range(N_TILES):
                cols = slice(b * N + n * P, b * N + (n + 1) * P)
                nc.tensor.matmul_mx(
                    out=y[n][:],
                    lhsT=wrec_codes[:, cols].bitcast(FP8X4),
                    lhsT_scale=wrec_plane[:, cols],
                    rhs=codes[:, 0:P3].bitcast(FP8X4),
                    rhs_scale=plane[:, 0:P3],
                    start=(b == 0),
                    stop=False,
                )
            for n in range(N_TILES):
                nc.tensor.matmul_mx(
                    out=y[n][:],
                    lhsT=wsq_codes[:, b, 2 * n * P : 2 * (n + 1) * P].bitcast(FP4X4),
                    lhsT_scale=wsq_plane[:, b, n * P : (n + 1) * P],
                    rhs=codes[:, P3 : 2 * P3].bitcast(FP8X4),
                    rhs_scale=plane[:, P3 : 2 * P3],
                    start=False,
                    stop=(b == R_PASSES - 1),
                )

        features(0)
        w1_rest = keep.tile([P, PACK - 1, P, PACK], BF16, name="w1_rest", align_bytes=64)
        round_w1(w1_rest, 0, 1, PACK)
        quantize_w1(w1_rest, 1, PACK)
        features(1)
        features(2)
        for i in range(SLICES + 2):
            if i < SLICES:
                pick_drills(i)
            if 0 <= i - 1 < SLICES:
                recruits(i - 1)
            if i < SLICES:
                larger(i)
            if 0 <= i - 2:
                squads(i - 2)
                if (i - 2) % PACK == PACK - 1:
                    round_level3((i - 2) // PACK)
            if i == 1:
                w1_second = keep.tile([P, PACK, P, PACK], BF16, name="w1_second", align_bytes=64)
                round_w1(w1_second, 1, 0, PACK)
                quantize_w1(w1_second, PACK, 2 * PACK)
            if i + H_SLOTS < SLICES:
                features(i + H_SLOTS)

        quantize_wrec(0, WREC_SPLIT)
        quantize_wrec(WREC_SPLIT, R_PASSES * N)
        for b in range(R_PASSES):
            second_stage(b)

        for n in range(N_TILES):
            result = ring.tile([P, P3], F32, name="result", bufs=N_TILES)
            nc.scalar.activation(result[:], y[n][:], ACT.Tanh)
            nc.sync.dma_start(out[n * P : (n + 1) * P, :], result[:])
